import numpy as np
import ml_dtypes


def mxq(x, axis, fmt="e4m3"):
    dtype, down = {"e4m3": (ml_dtypes.float8_e4m3fn, 7), "e5m2": (ml_dtypes.float8_e5m2, 14)}[fmt]
    v = np.moveaxis(np.asarray(x, np.float32).astype(ml_dtypes.bfloat16).astype(np.float64), axis, -1)
    blocks = v.reshape(v.shape[:-1] + (-1, 32))
    amax = np.abs(blocks).max(-1, keepdims=True)
    byte = np.maximum(np.where(amax > 0, np.frexp(amax)[1] - 1 + 127, 0) - down, 1)
    scale = np.exp2(byte - 127.0)
    codes = (blocks / scale).astype(np.float32).astype(dtype).astype(np.float64)
    return np.moveaxis((codes * scale).reshape(v.shape), -1, axis)


WIDE = False


def mx_kscale(k):
    if not WIDE:
        return np.ones(k)
    levels = np.array([10, -10, 5, -5, 0])
    if k % 512:
        return np.exp2(np.random.permutation(np.resize(levels, k // 32))).repeat(32)
    a = np.empty((k // 512, 16))
    for p in range(k // 512):
        a[p, :8] = np.random.permutation(np.resize(levels, 8))
        for g in range(8):
            far = levels[np.abs(levels - a[p, g]) >= 10]
            a[p, g + 8] = far[np.random.randint(len(far))]
    return np.exp2(a.ravel()).repeat(32)


BF16 = ml_dtypes.bfloat16


def bf(x):
    return np.asarray(x, np.float32).astype(BF16)


def f64(x):
    return np.asarray(x).astype(np.float64)


E2M1 = np.array([0.0, 0.5, 1.0, 1.5, 2.0, 3.0, 4.0, 6.0, -0.0, -0.5, -1.0, -1.5, -2.0, -3.0, -4.0, -6.0])


def pack_weight(w, fmt):
    k, n = w.shape
    w = f64(bf(w)).reshape(k // 32, 32, n)
    amax = np.abs(w).max(1)
    if fmt == "e4m3":
        byte = np.frexp(amax)[1] - 1 + 127 - 7
    else:
        mant, ex = np.frexp(amax / 6.0)
        byte = np.where(mant > 0.5, ex, ex - 1) + 127
    byte = np.clip(np.where(amax > 0, byte, 1), 1, 254)
    scaled = (w * np.exp2(127.0 - byte)[:, None, :]).reshape(k, n).astype(np.float32)
    by_word = np.ascontiguousarray(scaled.reshape(k // 512, 128, 4, n).transpose(0, 1, 3, 2))
    if fmt == "e4m3":
        words = by_word.astype(ml_dtypes.float8_e4m3fn).view(np.uint8)
    else:
        c = by_word.astype(ml_dtypes.float4_e2m1fn).view(np.uint8) & 0xF
        words = c[..., 0::2] | (c[..., 1::2] << 4)
    return np.ascontiguousarray(words), np.ascontiguousarray(byte.astype(np.uint8).reshape(k // 512, 16, n))


def unpack_weight(words, scales, fmt):
    g, p, n, _ = words.shape
    if fmt == "e4m3":
        vals = np.ascontiguousarray(words).view(ml_dtypes.float8_e4m3fn).astype(np.float64)
    else:
        nib = np.empty((g, p, n, 4), np.uint8)
        nib[..., 0::2] = words & 0xF
        nib[..., 1::2] = words >> 4
        vals = E2M1[nib]
    vals = vals * np.repeat(np.exp2(scales.astype(np.float64) - 127.0), 8, axis=1)[..., None]
    return vals.transpose(0, 1, 3, 2).reshape(g * 512, n)
def pack4(w):
    words, scales = pack_weight(w, "e2m1")
    return words.reshape(words.shape[0], 128, -1), scales


def unpack4(words, scales):
    return unpack_weight(words.reshape(words.shape[0], 128, -1, 2), scales, "e2m1")


M, K, N = 768, 2048, 1024


def setup_inputs():
    s = mx_kscale(K)
    ramp = 4.0 * (np.arange(N)[None, :] / N - np.arange(K)[:, None] / K) / K
    far = np.random.standard_normal((K, N)) / np.sqrt(K) + ramp
    near = np.random.standard_normal((K, N)) / np.sqrt(K) + ramp
    far_words, far_scales = pack4(far / s[:, None])
    near_words, near_scales = pack_weight(near / s[:, None], "e4m3")
    return {"logits": bf(2.0 * np.random.standard_normal((M, K))),
            "r": bf((1.0 + 0.1 * np.random.standard_normal(K)) * s),
            "far_words": far_words,
            "far_scales": far_scales,
            "near_words": near_words,
            "near_scales": near_scales,
            "mix": bf(2.0 * np.random.standard_normal((K, N)) / np.sqrt(K) / s[:, None])}


def reference(logits, r, far_words, far_scales, near_words, near_scales, mix):
    gate = f64(r) / (1.0 + np.exp(-f64(logits)))
    gq = mxq(gate, 1, "e4m3")
    far = gq @ unpack4(far_words, far_scales)
    near = gq @ unpack_weight(near_words, near_scales, "e4m3")
    m = gq @ mxq(f64(mix), 0, "e4m3")
    return near + np.tanh(m) * far

@@ -1,0 +1,363 @@
+from contextlib import ExitStack
+
+import concourse.mybir as mybir
+from concourse.masks import make_identity
+
+M, K, N = 768, 2048, 1024
+FLOPS = 3 * 2 * M * K * N
+
+F32 = mybir.dt.float32
+BF16 = mybir.dt.bfloat16
+I32 = mybir.dt.int32
+U32 = mybir.dt.uint32
+U8 = mybir.dt.uint8
+FP8X4 = mybir.dt.float8_e4m3fn_x4
+FP4X4 = mybir.dt.float4_e2m1fn_x4
+ACT = mybir.ActivationFunctionType
+ALU = mybir.AluOpType
+
+P = 128
+PACK = 4
+K_PASS = P * PACK
+PASSES = K // K_PASS
+N_HALF = 512
+BANKS = 8
+
+
+def tile_contextual_position_gates_s10_kernel(
+    tc, logits, r, far_words, far_scales, near_words, near_scales, mix, out
+):
+    nc = tc.nc
+    with ExitStack() as ctx:
+        keep = ctx.enter_context(tc.tile_pool(name="keep", bufs=1))
+        stage = ctx.enter_context(tc.tile_pool(name="stage", bufs=3))
+        psum = ctx.enter_context(tc.psum_pool(name="psum", bufs=1))
+        ctx.enter_context(tc.manual_schedule())
+
+        banks_taken = []
+
+        def next_bank():
+            tag = "bank%d" % (len(banks_taken) % BANKS)
+            bank = psum.tile([P, N_HALF], F32, name=tag, tag=tag)
+            banks_taken.append(bank)
+            return bank
+
+        def cols(h):
+            return slice(h * N_HALF, (h + 1) * N_HALF)
+
+        ident = keep.tile([P, P], F32, name="ident")
+        make_identity(nc, ident[:])
+
+        far_sc = [keep.tile([P, PASSES, N_HALF], U8, name="far_sc%d" % h, align_bytes=64) for h in range(2)]
+        near_sc = keep.tile([P, N], U8, name="near_sc", align_bytes=64)
+        for h in range(2):
+            nc.vector.memset(far_sc[h][:].bitcast(I32), 0)
+        nc.vector.memset(near_sc[:].bitcast(I32), 0)
+
+        logit_sb = {}
+        far_sb = {}
+        near_sb = {}
+        mix_raw = {}
+
+        def load_logits(m, pieces):
+            width = K // pieces
+            for i in range(pieces):
+                piece = keep.tile([P, width], BF16, name="logits%d_%d" % (m, i))
+                nc.sync.dma_start(out=piece[:], in_=logits[m * P : (m + 1) * P, i * width : (i + 1) * width])
+                for j in range(2 // pieces):
+                    logit_sb[(m, i + j)] = piece[:, j * (K // 2) : (j + 1) * (K // 2)]
+
+        def load_far(h):
+            for row in range(4):
+                nc.sync.dma_start(
+                    out=far_sc[h][row:P:32, :, :].bitcast(I32),
+                    in_=far_scales[:, row:16:4, cols(h)].rearrange("g q n -> q g n").bitcast(I32),
+                )
+            far_sb[h] = keep.tile([P, PASSES, 2 * N_HALF], U8, name="far%d" % h, align_bytes=64)
+            nc.sync.dma_start(
+                out=far_sb[h][:].bitcast(I32),
+                in_=far_words[:, :, 2 * h * N_HALF : 2 * (h + 1) * N_HALF].rearrange("g p n -> p g n").bitcast(I32),
+            )
+
+        def load_near_scales():
+            for q in range(4):
+                nc.sync.dma_start(
+                    out=near_sc[32 * q : 32 * q + 16, :].bitcast(I32),
+                    in_=near_scales[:, 4 * q : 4 * q + 4, :].bitcast(I32),
+                )
+
+        def load_near(h):
+            near_sb[h] = keep.tile([P, PASSES, N_HALF], U32, name="near%d" % h, align_bytes=64)
+            nc.sync.dma_start(
+                out=near_sb[h][:].bitcast(I32),
+                in_=near_words[:, :, cols(h), :].rearrange("g p n t -> p g (n t)").bitcast(I32),
+            )
+
+        def load_mix(h, g):
+            mix_raw[(h, g)] = keep.tile([P, PACK, N_HALF], BF16, name="mix%d_%d" % (h, g))
+            nc.sync.dma_start(
+                out=mix_raw[(h, g)][:],
+                in_=mix[g * K_PASS : (g + 1) * K_PASS, cols(h)].rearrange("(p t) n -> p t n", t=PACK),
+            )
+
+        r_sb = keep.tile([P, PASSES, PACK], BF16, name="r_sb")
+        load_logits(0, 2)
+        nc.sync.dma_start(out=r_sb[:], in_=r.rearrange("(g p t) -> p g t", p=P, t=PACK))
+        load_logits(1, 1)
+        load_far(0)
+        load_far(1)
+        load_near_scales()
+        load_logits(2, 1)
+        load_near(0)
+        load_near(1)
+        load_mix(0, 0)
+        load_logits(3, 1)
+        for g in range(1, PASSES):
+            load_mix(0, g)
+        load_logits(4, 1)
+        for g in range(PASSES):
+            load_mix(1, g)
+        load_logits(5, 1)
+
+        sig = {}
+        gate_bf = {}
+        gate_codes = {}
+        gate_sc = {}
+
+        def turn_and_sigmoid(m):
+            turned = []
+            for b in range(2):
+                words = logit_sb[(m, b)].bitcast(F32)
+                bank = next_bank()
+                for u in range(2):
+                    for g in range(2):
+                        slot = 2 * u + g
+                        nc.tensor.transpose(
+                            bank[:, slot * P : (slot + 1) * P], words[:, 2 * P * g + u : 2 * P * (g + 1) : 2], ident[:]
+                        )
+                turned.append(bank)
+            return turned
+
+        def sigmoid(m, turned):
+            for b in range(2):
+                sig[(m, b)] = stage.tile([P, 2 * P, 2, 2], F32, name="sig", tag="sig")
+                nc.scalar.activation(
+                    out=sig[(m, b)][:],
+                    in_=turned[b][:].bitcast(BF16).rearrange("p (u c e) -> p c u e", u=2, e=2),
+                    func=ACT.Sigmoid,
+                )
+
+        def weigh(m, b):
+            gate_bf[(m, b)] = stage.tile([P, 2, P, PACK], BF16, name="gate_bf", tag="gate_bf", align_bytes=64)
+            nc.vector.tensor_tensor(
+                out=gate_bf[(m, b)][:],
+                in0=sig[(m, b)][:].rearrange("p (g c) u e -> p g c (u e)", g=2),
+                in1=r_sb[:, 2 * b : 2 * b + 2, :].unsqueeze(2).to_broadcast([P, 2, P, PACK]),
+                op=ALU.mult,
+            )
+
+        def quantize_gate(m, b):
+            gate_codes[(m, b)] = keep.tile([P, 2 * P], U32, name="gate_codes%d_%d" % (m, b), align_bytes=64)
+            gate_sc[(m, b)] = keep.tile([P, 2 * P], U8, name="gate_sc%d_%d" % (m, b), align_bytes=64)
+            nc.vector.quantize_mx(
+                out=gate_codes[(m, b)][:].bitcast(FP8X4),
+                scales=gate_sc[(m, b)][:],
+                in_=gate_bf[(m, b)][:].rearrange("p g c t -> p (g c t)"),
+            )
+
+        woven = {}
+        mix_codes = {}
+        mix_sc = {}
+
+        def weave(h, g, copy):
+            woven[(h, g)] = stage.tile([P, N_HALF, PACK], BF16, name="woven", tag="woven", align_bytes=64)
+            copy(
+                out=woven[(h, g)][:].rearrange("p (c i) t -> p c t i", i=4),
+                in_=mix_raw[(h, g)][:].rearrange("p t (c i) -> p c t i", i=4),
+            )
+
+        def quantize_mix(h, g):
+            mix_codes[(h, g)] = keep.tile([P, N_HALF], U32, name="mix_codes%d_%d" % (h, g), align_bytes=64)
+            mix_sc[(h, g)] = keep.tile([P, N_HALF], U8, name="mix_sc%d_%d" % (h, g), align_bytes=64)
+            nc.vector.quantize_mx(
+                out=mix_codes[(h, g)][:].bitcast(FP8X4),
+                scales=mix_sc[(h, g)][:],
+                in_=woven[(h, g)][:].rearrange("p c t -> p (c t)"),
+            )
+
+        sums = {}
+
+        def product(kind, m, h, lo=0, hi=N_HALF):
+            bank = next_bank()
+            for g in range(PASSES):
+                if kind == "far":
+                    rhs = far_sb[h][:, g, 2 * lo : 2 * hi].bitcast(FP4X4)
+                    rhs_scale = far_sc[h][:, g, lo:hi]
+                elif kind == "near":
+                    rhs = near_sb[h][:, g, lo:hi].bitcast(FP8X4)
+                    rhs_scale = near_sc[4 * g : P, h * N_HALF + lo : h * N_HALF + hi]
+                else:
+                    rhs = mix_codes[(h, g)][:, lo:hi].bitcast(FP8X4)
+                    rhs_scale = mix_sc[(h, g)][:, lo:hi]
+                c = slice((g % 2) * P, (g % 2 + 1) * P)
+                nc.tensor.matmul_mx(
+                    out=bank[:, : hi - lo],
+                    lhsT=gate_codes[(m, g // 2)][:, c].bitcast(FP8X4),
+                    lhsT_scale=gate_sc[(m, g // 2)][:, c],
+                    rhs=rhs,
+                    rhs_scale=rhs_scale,
+                    start=(g == 0),
+                    stop=(g == PASSES - 1),
+                )
+            sums[(kind, m, h)] = bank[:, : hi - lo]
+
+        def park(kind, m, h):
+            parked = keep.tile([P, N_HALF], F32, name="parked_%s%d_%d" % (kind, m, h))
+            nc.scalar.copy(out=parked[:], in_=sums[(kind, m, h)])
+            sums[(kind, m, h)] = parked[:]
+
+        result = {}
+
+        def tanh(m, h):
+            result[(m, h)] = keep.tile([P, N_HALF], F32, name="result%d_%d" % (m, h))
+            nc.scalar.activation(out=result[(m, h)][:], in_=sums[("mix", m, h)], func=ACT.Tanh)
+
+        def times_far(m, h):
+            nc.vector.tensor_tensor(
+                out=result[(m, h)][:], in0=sums[("far", m, h)], in1=result[(m, h)][:], op=ALU.mult
+            )
+
+        def plus_near(m, h, lo=0, hi=N_HALF):
+            part = result[(m, h)][:, lo:hi]
+            nc.vector.tensor_tensor(out=part, in0=sums[("near", m, h)], in1=part, op=ALU.add)
+            nc.sync.dma_start(out=out[m * P : (m + 1) * P, h * N_HALF + lo : h * N_HALF + hi], in_=part)
+
+        on_vector = nc.vector.tensor_copy
+        on_scalar = nc.scalar.copy
+
+        t0 = turn_and_sigmoid(0)
+        sigmoid(0, t0)
+        t1 = turn_and_sigmoid(1)
+        sigmoid(1, t1)
+        for m in range(2):
+            for b in range(2):
+                weigh(m, b)
+                quantize_gate(m, b)
+        product("far", 0, 0)
+        product("far", 0, 1)
+        park("far", 0, 0)
+        park("far", 0, 1)
+        t2 = turn_and_sigmoid(2)
+        sigmoid(2, t2)
+        product("far", 1, 0)
+        product("far", 1, 1)
+        weigh(2, 0)
+        weigh(2, 1)
+        quantize_gate(2, 0)
+        quantize_gate(2, 1)
+        park("far", 1, 0)
+        park("far", 1, 1)
+        product("near", 0, 0)
+        product("near", 1, 0)
+        park("near", 0, 0)
+        park("near", 1, 0)
+        product("near", 0, 1)
+        product("near", 1, 1)
+        park("near", 0, 1)
+        weave(0, 0, on_vector)
+        quantize_mix(0, 0)
+        t3 = turn_and_sigmoid(3)
+        park("near", 1, 1)
+        sigmoid(3, t3)
+        weave(0, 1, on_vector)
+        quantize_mix(0, 1)
+        product("far", 2, 0)
+        product("far", 2, 1)
+        weigh(3, 0)
+        weigh(3, 1)
+        park("far", 2, 0)
+        park("far", 2, 1)
+        quantize_gate(3, 0)
+        quantize_gate(3, 1)
+        product("near", 2, 0)
+        product("near", 2, 1)
+        weave(0, 2, on_scalar)
+        weave(0, 3, on_vector)
+        park("near", 2, 0)
+        park("near", 2, 1)
+        quantize_mix(0, 3)
+        quantize_mix(0, 2)
+        t4 = turn_and_sigmoid(4)
+        sigmoid(4, t4)
+        weave(1, 0, on_vector)
+        product("far", 3, 0)
+        product("near", 3, 0)
+        product("mix", 3, 0)
+        weigh(4, 0)
+        weigh(4, 1)
+        tanh(3, 0)
+        quantize_mix(1, 0)
+        quantize_gate(4, 0)
+        quantize_gate(4, 1)
+        weave(1, 1, on_scalar)
+        product("mix", 0, 0)
+        product("mix", 1, 0)
+        times_far(3, 0)
+        weave(1, 2, on_vector)
+        plus_near(3, 0)
+        tanh(0, 0)
+        tanh(1, 0)
+        product("mix", 2, 0)
+        tanh(2, 0)
+        quantize_mix(1, 1)
+        quantize_mix(1, 2)
+        weave(1, 3, on_scalar)
+        product("mix", 4, 0)
+        tanh(4, 0)
+        product("far", 4, 0)
+        product("near", 4, 0)
+        times_far(0, 0)
+        times_far(1, 0)
+        plus_near(0, 0)
+        plus_near(1, 0)
+        quantize_mix(1, 3)
+        times_far(4, 0)
+        t5 = turn_and_sigmoid(5)
+        sigmoid(5, t5)
+        plus_near(4, 0)
+        product("mix", 3, 1)
+        product("far", 3, 1)
+        product("near", 3, 1)
+        tanh(3, 1)
+        weigh(5, 0)
+        times_far(3, 1)
+        weigh(5, 1)
+        plus_near(3, 1)
+        quantize_gate(5, 0)
+        quantize_gate(5, 1)
+        product("mix", 0, 1)
+        tanh(0, 1)
+        product("mix", 4, 1)
+        times_far(2, 0)
+        tanh(4, 1)
+        times_far(0, 1)
+        plus_near(2, 0)
+        plus_near(0, 1)
+        product("far", 4, 1)
+        product("near", 4, 1)
+        times_far(4, 1)
+        for early, h in ((1, 0), (2, 1)):
+            product("mix", early, 1)
+            plus_near(4 if h == 0 else 5, 1 - h)
+            tanh(early, 1)
+            product("mix", 5, h)
+            times_far(early, 1)
+            tanh(5, h)
+            plus_near(early, 1)
+            product("far", 5, h)
+            times_far(5, h)
+            if h == 0:
+                product("near", 5, h)
+        for lo in (0, N_HALF // 2):
+            product("near", 5, 1, lo, lo + N_HALF // 2)
+            plus_near(5, 1, lo, lo + N_HALF // 2)

@@ -48,10 +48,9 @@ def tile_contextual_position_gates_s10_kernel(
         ident = keep.tile([P, P], F32, name="ident")
         make_identity(nc, ident[:])
 
-        far_sc = [keep.tile([P, PASSES, N_HALF], U8, name="far_sc%d" % h, align_bytes=64) for h in range(2)]
+        far_sc = keep.tile([P, PASSES, N], U8, name="far_sc", align_bytes=64)
         near_sc = keep.tile([P, N], U8, name="near_sc", align_bytes=64)
-        for h in range(2):
-            nc.vector.memset(far_sc[h][:].bitcast(I32), 0)
+        nc.vector.memset(far_sc[:].bitcast(I32), 0)
         nc.vector.memset(near_sc[:].bitcast(I32), 0)
 
         logit_sb = {}
@@ -67,16 +66,18 @@ def tile_contextual_position_gates_s10_kernel(
                 for j in range(2 // pieces):
                     logit_sb[(m, i + j)] = piece[:, j * (K // 2) : (j + 1) * (K // 2)]
 
-        def load_far(h):
+        def load_far_scales():
             for row in range(4):
                 nc.sync.dma_start(
-                    out=far_sc[h][row:P:32, :, :].bitcast(I32),
-                    in_=far_scales[:, row:16:4, cols(h)].rearrange("g q n -> q g n").bitcast(I32),
+                    out=far_sc[row:P:32, :, :].bitcast(I32),
+                    in_=far_scales[:, row:16:4, :].rearrange("g q n -> q g n").bitcast(I32),
                 )
-            far_sb[h] = keep.tile([P, PASSES, 2 * N_HALF], U8, name="far%d" % h, align_bytes=64)
+
+        def load_far(b):
+            far_sb[b] = keep.tile([P, 2, 2 * N], U8, name="far%d" % b, align_bytes=64)
             nc.sync.dma_start(
-                out=far_sb[h][:].bitcast(I32),
-                in_=far_words[:, :, 2 * h * N_HALF : 2 * (h + 1) * N_HALF].rearrange("g p n -> p g n").bitcast(I32),
+                out=far_sb[b][:].bitcast(I32),
+                in_=far_words[2 * b : 2 * b + 2].rearrange("g p n -> p g n").bitcast(I32),
             )
 
         def load_near_scales():
@@ -100,70 +101,95 @@ def tile_contextual_position_gates_s10_kernel(
                 in_=mix[g * K_PASS : (g + 1) * K_PASS, cols(h)].rearrange("(p t) n -> p t n", t=PACK),
             )
 
-        r_sb = keep.tile([P, PASSES, PACK], BF16, name="r_sb")
+        r_sb = keep.tile([P, PASSES, 16], BF16, name="r_sb")
         load_logits(0, 2)
-        nc.sync.dma_start(out=r_sb[:], in_=r.rearrange("(g p t) -> p g t", p=P, t=PACK))
+        nc.sync.dma_start(out=r_sb[:, :, :PACK], in_=r.rearrange("(g p t) -> p g t", p=P, t=PACK))
         load_logits(1, 1)
+        load_far_scales()
         load_far(0)
         load_far(1)
-        load_near_scales()
         load_logits(2, 1)
+        load_near_scales()
         load_near(0)
-        load_near(1)
         load_mix(0, 0)
         load_logits(3, 1)
-        for g in range(1, PASSES):
-            load_mix(0, g)
+        load_mix(0, 1)
+        load_near(1)
+        load_mix(0, 2)
+        load_mix(0, 3)
         load_logits(4, 1)
         for g in range(PASSES):
             load_mix(1, g)
         load_logits(5, 1)
 
+        sorted_words = {}
+        turned = {}
         sig = {}
         gate_bf = {}
         gate_codes = {}
         gate_sc = {}
 
-        def turn_and_sigmoid(m):
-            turned = []
+        def sort_words(m):
             for b in range(2):
-                words = logit_sb[(m, b)].bitcast(F32)
-                bank = next_bank()
-                for u in range(2):
-                    for g in range(2):
-                        slot = 2 * u + g
-                        nc.tensor.transpose(
-                            bank[:, slot * P : (slot + 1) * P], words[:, 2 * P * g + u : 2 * P * (g + 1) : 2], ident[:]
-                        )
-                turned.append(bank)
-            return turned
-
-        def sigmoid(m, turned):
-            for b in range(2):
-                sig[(m, b)] = stage.tile([P, 2 * P, 2, 2], F32, name="sig", tag="sig")
-                nc.scalar.activation(
-                    out=sig[(m, b)][:],
-                    in_=turned[b][:].bitcast(BF16).rearrange("p (u c e) -> p c u e", u=2, e=2),
-                    func=ACT.Sigmoid,
+                ordered = stage.tile([P, 2, 2, P], F32, name="ordered", tag="ordered")
+                nc.scalar.copy(
+                    out=ordered[:], in_=logit_sb[(m, b)].bitcast(F32).rearrange("p (g c u) -> p u g c", g=2, u=2)
                 )
+                sorted_words[(m, b)] = ordered
 
-        def weigh(m, b):
-            gate_bf[(m, b)] = stage.tile([P, 2, P, PACK], BF16, name="gate_bf", tag="gate_bf", align_bytes=64)
+        def turn(m, g0, count):
+            bank = next_bank()
+            for u in range(2):
+                for i in range(count):
+                    g = g0 + i
+                    if (m, g // 2) in sorted_words:
+                        words = sorted_words[(m, g // 2)][:, u, g % 2, :]
+                    else:
+                        words = logit_sb[(m, g // 2)].bitcast(F32)[:, 2 * P * (g % 2) + u : 2 * P * (g % 2 + 1) : 2]
+                    slot = count * u + i
+                    nc.tensor.transpose(bank[:, slot * P : (slot + 1) * P], words, ident[:])
+            turned[(m, g0)] = bank[:, : 2 * count * P]
+
+        def sigmoid(m, g0, count):
+            sig[(m, g0)] = stage.tile([P, count * P, 2, 2], F32, name="sig", tag="sig", bufs=4)
+            nc.scalar.activation(
+                out=sig[(m, g0)][:],
+                in_=turned[(m, g0)].bitcast(BF16).rearrange("p (u c e) -> p c u e", u=2, e=2),
+                func=ACT.Sigmoid,
+            )
+
+        def weigh(m, g0, count):
+            gate_bf[(m, g0)] = stage.tile([P, count, P, PACK], BF16, name="gate_bf", tag="gate_bf", align_bytes=64)
             nc.vector.tensor_tensor(
-                out=gate_bf[(m, b)][:],
-                in0=sig[(m, b)][:].rearrange("p (g c) u e -> p g c (u e)", g=2),
-                in1=r_sb[:, 2 * b : 2 * b + 2, :].unsqueeze(2).to_broadcast([P, 2, P, PACK]),
+                out=gate_bf[(m, g0)][:],
+                in0=sig[(m, g0)][:].rearrange("p (g c) u e -> p g c (u e)", g=count),
+                in1=r_sb[:, g0 : g0 + count, :PACK].unsqueeze(2).to_broadcast([P, count, P, PACK]),
                 op=ALU.mult,
             )
 
-        def quantize_gate(m, b):
-            gate_codes[(m, b)] = keep.tile([P, 2 * P], U32, name="gate_codes%d_%d" % (m, b), align_bytes=64)
-            gate_sc[(m, b)] = keep.tile([P, 2 * P], U8, name="gate_sc%d_%d" % (m, b), align_bytes=64)
+        def quantize_gate(m, g0, count):
+            codes = keep.tile([P, count * P], U32, name="gate_codes%d_%d" % (m, g0), align_bytes=64)
+            scales = keep.tile([P, count * P], U8, name="gate_sc%d_%d" % (m, g0), align_bytes=64)
             nc.vector.quantize_mx(
-                out=gate_codes[(m, b)][:].bitcast(FP8X4),
-                scales=gate_sc[(m, b)][:],
-                in_=gate_bf[(m, b)][:].rearrange("p g c t -> p (g c t)"),
+                out=codes[:].bitcast(FP8X4),
+                scales=scales[:],
+                in_=gate_bf[(m, g0)][:].rearrange("p g c t -> p (g c t)"),
             )
+            for i in range(count):
+                gate_codes[(m, g0 + i)] = codes[:, i * P : (i + 1) * P]
+                gate_sc[(m, g0 + i)] = scales[:, i * P : (i + 1) * P]
+
+        def turn_and_sigmoid(m):
+            for g0 in (0, 2):
+                turn(m, g0, 2)
+            for g0 in (0, 2):
+                sigmoid(m, g0, 2)
+
+        def weigh_and_quantize(m):
+            for g0 in (0, 2):
+                weigh(m, g0, 2)
+            for g0 in (0, 2):
+                quantize_gate(m, g0, 2)
 
         woven = {}
         mix_codes = {}
@@ -187,29 +213,29 @@ def tile_contextual_position_gates_s10_kernel(
 
         sums = {}
 
-        def product(kind, m, h, lo=0, hi=N_HALF):
-            bank = next_bank()
-            for g in range(PASSES):
+        def product(kind, m, h, lo=0, hi=N_HALF, passes=range(PASSES)):
+            if passes[0] == 0:
+                sums[(kind, m, h)] = next_bank()[:, : hi - lo]
+            first, last = h * N_HALF + lo, h * N_HALF + hi
+            for g in passes:
                 if kind == "far":
-                    rhs = far_sb[h][:, g, 2 * lo : 2 * hi].bitcast(FP4X4)
-                    rhs_scale = far_sc[h][:, g, lo:hi]
+                    rhs = far_sb[g // 2][:, g % 2, 2 * first : 2 * last].bitcast(FP4X4)
+                    rhs_scale = far_sc[:, g, first:last]
                 elif kind == "near":
                     rhs = near_sb[h][:, g, lo:hi].bitcast(FP8X4)
-                    rhs_scale = near_sc[4 * g : P, h * N_HALF + lo : h * N_HALF + hi]
+                    rhs_scale = near_sc[4 * g : P, first:last]
                 else:
                     rhs = mix_codes[(h, g)][:, lo:hi].bitcast(FP8X4)
                     rhs_scale = mix_sc[(h, g)][:, lo:hi]
-                c = slice((g % 2) * P, (g % 2 + 1) * P)
                 nc.tensor.matmul_mx(
-                    out=bank[:, : hi - lo],
-                    lhsT=gate_codes[(m, g // 2)][:, c].bitcast(FP8X4),
-                    lhsT_scale=gate_sc[(m, g // 2)][:, c],
+                    out=sums[(kind, m, h)],
+                    lhsT=gate_codes[(m, g)].bitcast(FP8X4),
+                    lhsT_scale=gate_sc[(m, g)],
                     rhs=rhs,
                     rhs_scale=rhs_scale,
                     start=(g == 0),
                     stop=(g == PASSES - 1),
                 )
-            sums[(kind, m, h)] = bank[:, : hi - lo]
 
         def park(kind, m, h):
             parked = keep.tile([P, N_HALF], F32, name="parked_%s%d_%d" % (kind, m, h))
@@ -235,129 +261,166 @@ def tile_contextual_position_gates_s10_kernel(
         on_vector = nc.vector.tensor_copy
         on_scalar = nc.scalar.copy
 
-        t0 = turn_and_sigmoid(0)
-        sigmoid(0, t0)
-        t1 = turn_and_sigmoid(1)
-        sigmoid(1, t1)
-        for m in range(2):
-            for b in range(2):
-                weigh(m, b)
-                quantize_gate(m, b)
-        product("far", 0, 0)
-        product("far", 0, 1)
+        turn(0, 0, 1)
+        turn(0, 1, 1)
+        turn(0, 2, 1)
+        turn(0, 3, 1)
+        sigmoid(0, 0, 1)
+        sigmoid(0, 1, 1)
+        sigmoid(0, 2, 1)
+        sigmoid(0, 3, 1)
+        turn(1, 0, 2)
+        turn(1, 2, 2)
+        sigmoid(1, 0, 2)
+        sigmoid(1, 2, 2)
+        weigh(0, 0, 1)
+        weigh(0, 1, 1)
+        quantize_gate(0, 0, 1)
+        weigh(0, 2, 1)
+        quantize_gate(0, 1, 1)
+        weigh(0, 3, 1)
+        quantize_gate(0, 2, 1)
+        weigh(1, 0, 2)
+        quantize_gate(0, 3, 1)
+        weigh(1, 2, 2)
+        quantize_gate(1, 0, 2)
+        quantize_gate(1, 2, 2)
+        product("far", 0, 0, passes=range(0, 2))
+        product("far", 0, 1, passes=range(0, 2))
+        product("far", 0, 0, passes=range(2, 4))
+        product("far", 0, 1, passes=range(2, 4))
+        sort_words(2)
         park("far", 0, 0)
         park("far", 0, 1)
-        t2 = turn_and_sigmoid(2)
-        sigmoid(2, t2)
+        turn(2, 0, 2)
+        turn(2, 2, 2)
+        sigmoid(2, 0, 2)
+        sigmoid(2, 2, 2)
         product("far", 1, 0)
         product("far", 1, 1)
-        weigh(2, 0)
-        weigh(2, 1)
-        quantize_gate(2, 0)
-        quantize_gate(2, 1)
+        weigh(2, 0, 2)
+        weigh(2, 2, 2)
+        quantize_gate(2, 0, 2)
+        quantize_gate(2, 2, 2)
         park("far", 1, 0)
         park("far", 1, 1)
         product("near", 0, 0)
         product("near", 1, 0)
+        sort_words(3)
         park("near", 0, 0)
         park("near", 1, 0)
-        product("near", 0, 1)
-        product("near", 1, 1)
-        park("near", 0, 1)
         weave(0, 0, on_vector)
-        quantize_mix(0, 0)
-        t3 = turn_and_sigmoid(3)
-        park("near", 1, 1)
-        sigmoid(3, t3)
         weave(0, 1, on_vector)
+        quantize_mix(0, 0)
         quantize_mix(0, 1)
+        turn(3, 0, 2)
+        turn(3, 2, 2)
+        sigmoid(3, 0, 2)
+        sigmoid(3, 2, 2)
         product("far", 2, 0)
         product("far", 2, 1)
-        weigh(3, 0)
-        weigh(3, 1)
+        weigh(3, 0, 2)
+        weigh(3, 2, 2)
+        quantize_gate(3, 0, 2)
+        quantize_gate(3, 2, 2)
         park("far", 2, 0)
         park("far", 2, 1)
-        quantize_gate(3, 0)
-        quantize_gate(3, 1)
         product("near", 2, 0)
-        product("near", 2, 1)
-        weave(0, 2, on_scalar)
-        weave(0, 3, on_vector)
+        product("near", 0, 1)
         park("near", 2, 0)
+        park("near", 0, 1)
+        product("near", 1, 1)
+        product("near", 2, 1)
+        weave(0, 2, on_vector)
+        weave(0, 3, on_vector)
+        sort_words(4)
+        park("near", 1, 1)
         park("near", 2, 1)
-        quantize_mix(0, 3)
         quantize_mix(0, 2)
-        t4 = turn_and_sigmoid(4)
-        sigmoid(4, t4)
+        quantize_mix(0, 3)
+        turn(4, 0, 2)
+        turn(4, 2, 2)
+        sigmoid(4, 0, 2)
+        sigmoid(4, 2, 2)
         weave(1, 0, on_vector)
+        weave(1, 1, on_scalar)
         product("far", 3, 0)
         product("near", 3, 0)
         product("mix", 3, 0)
-        weigh(4, 0)
-        weigh(4, 1)
+        weigh(4, 0, 2)
+        weigh(4, 2, 2)
         tanh(3, 0)
-        quantize_mix(1, 0)
-        quantize_gate(4, 0)
-        quantize_gate(4, 1)
-        weave(1, 1, on_scalar)
+        quantize_gate(4, 0, 2)
+        quantize_gate(4, 2, 2)
         product("mix", 0, 0)
         product("mix", 1, 0)
-        times_far(3, 0)
-        weave(1, 2, on_vector)
-        plus_near(3, 0)
         tanh(0, 0)
         tanh(1, 0)
+        weave(1, 2, on_vector)
+        times_far(3, 0)
+        quantize_mix(1, 0)
+        plus_near(3, 0)
+        quantize_mix(1, 1)
         product("mix", 2, 0)
         tanh(2, 0)
-        quantize_mix(1, 1)
-        quantize_mix(1, 2)
         weave(1, 3, on_scalar)
         product("mix", 4, 0)
-        tanh(4, 0)
         product("far", 4, 0)
         product("near", 4, 0)
         times_far(0, 0)
         times_far(1, 0)
+        tanh(4, 0)
+        quantize_mix(1, 2)
         plus_near(0, 0)
         plus_near(1, 0)
-        quantize_mix(1, 3)
         times_far(4, 0)
-        t5 = turn_and_sigmoid(5)
-        sigmoid(5, t5)
+        quantize_mix(1, 3)
+        sort_words(5)
         plus_near(4, 0)
-        product("mix", 3, 1)
         product("far", 3, 1)
         product("near", 3, 1)
+        product("mix", 3, 1)
+        turn(5, 0, 2)
+        turn(5, 2, 2)
         tanh(3, 1)
-        weigh(5, 0)
+        sigmoid(5, 0, 2)
+        sigmoid(5, 2, 2)
+        times_far(2, 0)
         times_far(3, 1)
-        weigh(5, 1)
+        plus_near(2, 0)
         plus_near(3, 1)
-        quantize_gate(5, 0)
-        quantize_gate(5, 1)
         product("mix", 0, 1)
         tanh(0, 1)
         product("mix", 4, 1)
-        times_far(2, 0)
+        weigh(5, 0, 2)
+        weigh(5, 2, 2)
         tanh(4, 1)
-        times_far(0, 1)
-        plus_near(2, 0)
-        plus_near(0, 1)
+        quantize_gate(5, 0, 2)
+        quantize_gate(5, 2, 2)
         product("far", 4, 1)
         product("near", 4, 1)
+        times_far(0, 1)
         times_far(4, 1)
-        for early, h in ((1, 0), (2, 1)):
-            product("mix", early, 1)
-            plus_near(4 if h == 0 else 5, 1 - h)
-            tanh(early, 1)
-            product("mix", 5, h)
-            times_far(early, 1)
-            tanh(5, h)
-            plus_near(early, 1)
-            product("far", 5, h)
-            times_far(5, h)
-            if h == 0:
-                product("near", 5, h)
+        plus_near(0, 1)
+        plus_near(4, 1)
+        product("mix", 1, 1)
+        tanh(1, 1)
+        product("mix", 2, 1)
+        tanh(2, 1)
+        times_far(1, 1)
+        product("mix", 5, 0)
+        tanh(5, 0)
+        times_far(2, 1)
+        plus_near(1, 1)
+        plus_near(2, 1)
+        product("far", 5, 0)
+        times_far(5, 0)
+        product("near", 5, 0)
+        product("mix", 5, 1)
+        plus_near(5, 0)
+        tanh(5, 1)
+        product("far", 5, 1)
+        times_far(5, 1)
         for lo in (0, N_HALF // 2):
             product("near", 5, 1, lo, lo + N_HALF // 2)
             plus_near(5, 1, lo, lo + N_HALF // 2)

@@ -22,6 +22,8 @@ K_PASS = P * PACK
 PASSES = K // K_PASS
 N_HALF = 512
 BANKS = 8
+WARM_N = 256
+WARM_PASSES = 6
 
 
 def tile_contextual_position_gates_s10_kernel(
@@ -34,19 +36,45 @@ def tile_contextual_position_gates_s10_kernel(
         psum = ctx.enter_context(tc.psum_pool(name="psum", bufs=1))
         ctx.enter_context(tc.manual_schedule())
 
-        banks_taken = []
+        free_banks = ["bank%d" % i for i in range(BANKS)]
+        bank_of = {}
 
-        def next_bank():
-            tag = "bank%d" % (len(banks_taken) % BANKS)
+        def take_bank(key):
+            tag = free_banks[0]
+            free_banks.remove(tag)
+            bank_of[key] = tag
             bank = psum.tile([P, N_HALF], F32, name=tag, tag=tag)
-            banks_taken.append(bank)
             return bank
+
+        def give_back(key):
+            if bank_of.get(key):
+                free_banks.append(bank_of[key])
+                bank_of[key] = None
 
         def cols(h):
             return slice(h * N_HALF, (h + 1) * N_HALF)
 
         ident = keep.tile([P, P], F32, name="ident")
         make_identity(nc, ident[:])
+
+        ones = keep.tile([P, PACK * WARM_N], BF16, name="ones", align_bytes=64)
+        warm_codes = keep.tile([P, WARM_N], U32, name="warm_codes", align_bytes=64)
+        warm_sc = keep.tile([P, WARM_N], U8, name="warm_sc", align_bytes=64)
+        nc.vector.memset(ones[:].bitcast(I32), 0x3F803F80)
+        nc.vector.quantize_mx(out=warm_codes[:].bitcast(FP8X4), scales=warm_sc[:], in_=ones[:])
+        warm_bank = take_bank("warm")
+
+        def keep_warm():
+            for i in range(WARM_PASSES):
+                nc.tensor.matmul_mx(
+                    out=warm_bank[:, :WARM_N],
+                    lhsT=warm_codes[:, :P].bitcast(FP8X4),
+                    lhsT_scale=warm_sc[:, :P],
+                    rhs=warm_codes[:].bitcast(FP8X4),
+                    rhs_scale=warm_sc[:],
+                    start=True,
+                    stop=True,
+                )
 
         far_sc = keep.tile([P, PASSES, N], U8, name="far_sc", align_bytes=64)
         near_sc = keep.tile([P, N], U8, name="near_sc", align_bytes=64)
@@ -105,19 +133,19 @@ def tile_contextual_position_gates_s10_kernel(
         load_logits(0, 2)
         nc.sync.dma_start(out=r_sb[:, :, :PACK], in_=r.rearrange("(g p t) -> p g t", p=P, t=PACK))
         load_logits(1, 1)
+        load_logits(2, 1)
         load_far_scales()
         load_far(0)
         load_far(1)
-        load_logits(2, 1)
-        load_near_scales()
-        load_near(0)
         load_mix(0, 0)
         load_logits(3, 1)
+        load_near_scales()
+        load_near(0)
         load_mix(0, 1)
         load_near(1)
         load_mix(0, 2)
-        load_mix(0, 3)
         load_logits(4, 1)
+        load_mix(0, 3)
         for g in range(PASSES):
             load_mix(1, g)
         load_logits(5, 1)
@@ -138,7 +166,7 @@ def tile_contextual_position_gates_s10_kernel(
                 sorted_words[(m, b)] = ordered
 
         def turn(m, g0, count):
-            bank = next_bank()
+            bank = take_bank(("turn", m, g0))
             for u in range(2):
                 for i in range(count):
                     g = g0 + i
@@ -157,6 +185,7 @@ def tile_contextual_position_gates_s10_kernel(
                 in_=turned[(m, g0)].bitcast(BF16).rearrange("p (u c e) -> p c u e", u=2, e=2),
                 func=ACT.Sigmoid,
             )
+            give_back(("turn", m, g0))
 
         def weigh(m, g0, count):
             gate_bf[(m, g0)] = stage.tile([P, count, P, PACK], BF16, name="gate_bf", tag="gate_bf", align_bytes=64)
@@ -215,7 +244,7 @@ def tile_contextual_position_gates_s10_kernel(
 
         def product(kind, m, h, lo=0, hi=N_HALF, passes=range(PASSES)):
             if passes[0] == 0:
-                sums[(kind, m, h)] = next_bank()[:, : hi - lo]
+                sums[(kind, m, h)] = take_bank((kind, m, h))[:, : hi - lo]
             first, last = h * N_HALF + lo, h * N_HALF + hi
             for g in passes:
                 if kind == "far":
@@ -241,26 +270,31 @@ def tile_contextual_position_gates_s10_kernel(
             parked = keep.tile([P, N_HALF], F32, name="parked_%s%d_%d" % (kind, m, h))
             nc.scalar.copy(out=parked[:], in_=sums[(kind, m, h)])
             sums[(kind, m, h)] = parked[:]
+            give_back((kind, m, h))
 
         result = {}
 
         def tanh(m, h):
             result[(m, h)] = keep.tile([P, N_HALF], F32, name="result%d_%d" % (m, h))
             nc.scalar.activation(out=result[(m, h)][:], in_=sums[("mix", m, h)], func=ACT.Tanh)
+            give_back(("mix", m, h))
 
         def times_far(m, h):
             nc.vector.tensor_tensor(
                 out=result[(m, h)][:], in0=sums[("far", m, h)], in1=result[(m, h)][:], op=ALU.mult
             )
+            give_back(("far", m, h))
 
         def plus_near(m, h, lo=0, hi=N_HALF):
             part = result[(m, h)][:, lo:hi]
             nc.vector.tensor_tensor(out=part, in0=sums[("near", m, h)], in1=part, op=ALU.add)
+            give_back(("near", m, h))
             nc.sync.dma_start(out=out[m * P : (m + 1) * P, h * N_HALF + lo : h * N_HALF + hi], in_=part)
 
         on_vector = nc.vector.tensor_copy
         on_scalar = nc.scalar.copy
 
+        keep_warm()
         turn(0, 0, 1)
         turn(0, 1, 1)
         turn(0, 2, 1)
@@ -269,6 +303,7 @@ def tile_contextual_position_gates_s10_kernel(
         sigmoid(0, 1, 1)
         sigmoid(0, 2, 1)
         sigmoid(0, 3, 1)
+        keep_warm()
         turn(1, 0, 2)
         turn(1, 2, 2)
         sigmoid(1, 0, 2)
@@ -285,99 +320,100 @@ def tile_contextual_position_gates_s10_kernel(
         weigh(1, 2, 2)
         quantize_gate(1, 0, 2)
         quantize_gate(1, 2, 2)
-        product("far", 0, 0, passes=range(0, 2))
-        product("far", 0, 1, passes=range(0, 2))
-        product("far", 0, 0, passes=range(2, 4))
-        product("far", 0, 1, passes=range(2, 4))
-        sort_words(2)
-        park("far", 0, 0)
-        park("far", 0, 1)
+        keep_warm()
         turn(2, 0, 2)
         turn(2, 2, 2)
         sigmoid(2, 0, 2)
         sigmoid(2, 2, 2)
-        product("far", 1, 0)
-        product("far", 1, 1)
+        keep_warm()
+        give_back("warm")
+        product("far", 0, 0, passes=range(0, 2))
+        product("far", 0, 1, passes=range(0, 2))
+        product("far", 0, 0, passes=range(2, 4))
+        product("far", 0, 1, passes=range(2, 4))
         weigh(2, 0, 2)
         weigh(2, 2, 2)
         quantize_gate(2, 0, 2)
         quantize_gate(2, 2, 2)
+        park("far", 0, 0)
+        park("far", 0, 1)
+        product("far", 1, 0)
+        product("far", 1, 1)
         park("far", 1, 0)
-        park("far", 1, 1)
-        product("near", 0, 0)
-        product("near", 1, 0)
         sort_words(3)
-        park("near", 0, 0)
-        park("near", 1, 0)
+        park("far", 1, 1)
         weave(0, 0, on_vector)
-        weave(0, 1, on_vector)
-        quantize_mix(0, 0)
-        quantize_mix(0, 1)
+        product("far", 2, 0)
         turn(3, 0, 2)
         turn(3, 2, 2)
         sigmoid(3, 0, 2)
         sigmoid(3, 2, 2)
-        product("far", 2, 0)
+        quantize_mix(0, 0)
         product("far", 2, 1)
+        park("far", 2, 0)
+        park("far", 2, 1)
         weigh(3, 0, 2)
         weigh(3, 2, 2)
         quantize_gate(3, 0, 2)
         quantize_gate(3, 2, 2)
-        park("far", 2, 0)
-        park("far", 2, 1)
+        product("near", 0, 0)
+        product("near", 1, 0)
         product("near", 2, 0)
-        product("near", 0, 1)
+        park("near", 0, 0)
+        park("near", 1, 0)
         park("near", 2, 0)
+        weave(0, 1, on_vector)
+        product("far", 3, 1)
+        product("near", 0, 1)
+        park("far", 3, 1)
         park("near", 0, 1)
-        product("near", 1, 1)
-        product("near", 2, 1)
+        quantize_mix(0, 1)
         weave(0, 2, on_vector)
-        weave(0, 3, on_vector)
+        product("near", 1, 1)
         sort_words(4)
         park("near", 1, 1)
-        park("near", 2, 1)
         quantize_mix(0, 2)
-        quantize_mix(0, 3)
+        product("near", 2, 1)
         turn(4, 0, 2)
         turn(4, 2, 2)
         sigmoid(4, 0, 2)
         sigmoid(4, 2, 2)
-        weave(1, 0, on_vector)
-        weave(1, 1, on_scalar)
+        weave(0, 3, on_vector)
+        park("near", 2, 1)
         product("far", 3, 0)
         product("near", 3, 0)
-        product("mix", 3, 0)
         weigh(4, 0, 2)
+        quantize_mix(0, 3)
         weigh(4, 2, 2)
-        tanh(3, 0)
+        weave(1, 0, on_scalar)
+        product("mix", 3, 0)
         quantize_gate(4, 0, 2)
         quantize_gate(4, 2, 2)
+        tanh(3, 0)
         product("mix", 0, 0)
         product("mix", 1, 0)
+        product("mix", 2, 0)
+        weave(1, 1, on_vector)
+        times_far(3, 0)
         tanh(0, 0)
         tanh(1, 0)
-        weave(1, 2, on_vector)
-        times_far(3, 0)
+        weave(1, 2, on_scalar)
         quantize_mix(1, 0)
         plus_near(3, 0)
         quantize_mix(1, 1)
-        product("mix", 2, 0)
         tanh(2, 0)
-        weave(1, 3, on_scalar)
         product("mix", 4, 0)
         product("far", 4, 0)
         product("near", 4, 0)
-        times_far(0, 0)
-        times_far(1, 0)
+        weave(1, 3, on_vector)
         tanh(4, 0)
-        quantize_mix(1, 2)
-        plus_near(0, 0)
-        plus_near(1, 0)
-        times_far(4, 0)
-        quantize_mix(1, 3)
         sort_words(5)
+        quantize_mix(1, 2)
+        quantize_mix(1, 3)
+        times_far(4, 0)
+        times_far(0, 0)
         plus_near(4, 0)
-        product("far", 3, 1)
+        plus_near(0, 0)
         product("near", 3, 1)
         product("mix", 3, 1)
         turn(5, 0, 2)
@@ -385,18 +421,20 @@ def tile_contextual_position_gates_s10_kernel(
         tanh(3, 1)
         sigmoid(5, 0, 2)
         sigmoid(5, 2, 2)
+        times_far(1, 0)
         times_far(2, 0)
-        times_far(3, 1)
+        plus_near(1, 0)
         plus_near(2, 0)
-        plus_near(3, 1)
         product("mix", 0, 1)
         tanh(0, 1)
-        product("mix", 4, 1)
+        times_far(3, 1)
         weigh(5, 0, 2)
+        plus_near(3, 1)
         weigh(5, 2, 2)
-        tanh(4, 1)
         quantize_gate(5, 0, 2)
         quantize_gate(5, 2, 2)
+        product("mix", 4, 1)
+        tanh(4, 1)
         product("far", 4, 1)
         product("near", 4, 1)
         times_far(0, 1)
@@ -407,15 +445,15 @@ def tile_contextual_position_gates_s10_kernel(
         tanh(1, 1)
         product("mix", 2, 1)
         tanh(2, 1)
-        times_far(1, 1)
         product("mix", 5, 0)
         tanh(5, 0)
+        times_far(1, 1)
         times_far(2, 1)
         plus_near(1, 1)
         plus_near(2, 1)
         product("far", 5, 0)
-        times_far(5, 0)
         product("near", 5, 0)
+        times_far(5, 0)
         product("mix", 5, 1)
         plus_near(5, 0)
         tanh(5, 1)

@@ -22,8 +22,15 @@ K_PASS = P * PACK
 PASSES = K // K_PASS
 N_HALF = 512
 BANKS = 8
+QUADRANT = 32
+R_PITCH = 16
+RUN = 4
+STAGE_BUFS = 3
+SIG_BUFS = 4
 WARM_N = 256
-WARM_PASSES = 6
+WARM_FIRST = 5
+WARM_BETWEEN = 4
+ONES_BF16_PAIR = 0x3F803F80
 
 
 def tile_contextual_position_gates_s10_kernel(
@@ -32,7 +39,7 @@ def tile_contextual_position_gates_s10_kernel(
     nc = tc.nc
     with ExitStack() as ctx:
         keep = ctx.enter_context(tc.tile_pool(name="keep", bufs=1))
-        stage = ctx.enter_context(tc.tile_pool(name="stage", bufs=3))
+        stage = ctx.enter_context(tc.tile_pool(name="stage", bufs=STAGE_BUFS))
         psum = ctx.enter_context(tc.psum_pool(name="psum", bufs=1))
         ctx.enter_context(tc.manual_schedule())
 
@@ -47,25 +54,22 @@ def tile_contextual_position_gates_s10_kernel(
             return bank
 
         def give_back(key):
-            if bank_of.get(key):
+            if bank_of[key]:
                 free_banks.append(bank_of[key])
                 bank_of[key] = None
 
         def cols(h):
             return slice(h * N_HALF, (h + 1) * N_HALF)
 
-        ident = keep.tile([P, P], F32, name="ident")
-        make_identity(nc, ident[:])
-
         ones = keep.tile([P, PACK * WARM_N], BF16, name="ones", align_bytes=64)
         warm_codes = keep.tile([P, WARM_N], U32, name="warm_codes", align_bytes=64)
         warm_sc = keep.tile([P, WARM_N], U8, name="warm_sc", align_bytes=64)
-        nc.vector.memset(ones[:].bitcast(I32), 0x3F803F80)
+        nc.vector.memset(ones[:].bitcast(I32), ONES_BF16_PAIR)
         nc.vector.quantize_mx(out=warm_codes[:].bitcast(FP8X4), scales=warm_sc[:], in_=ones[:])
         warm_bank = take_bank("warm")
 
-        def keep_warm():
-            for i in range(WARM_PASSES):
+        def keep_warm(count):
+            for i in range(count):
                 nc.tensor.matmul_mx(
                     out=warm_bank[:, :WARM_N],
                     lhsT=warm_codes[:, :P].bitcast(FP8X4),
@@ -76,12 +80,16 @@ def tile_contextual_position_gates_s10_kernel(
                     stop=True,
                 )
 
+        ident = keep.tile([P, P], F32, name="ident")
+        nc.vector.memset(ident[:], 0.0)
+        make_identity(nc, ident[:], nomemset=True)
+
         far_sc = keep.tile([P, PASSES, N], U8, name="far_sc", align_bytes=64)
         near_sc = keep.tile([P, N], U8, name="near_sc", align_bytes=64)
         nc.vector.memset(far_sc[:].bitcast(I32), 0)
         nc.vector.memset(near_sc[:].bitcast(I32), 0)
 
-        logit_sb = {}
+        logit_words = {}
         far_sb = {}
         near_sb = {}
         mix_raw = {}
@@ -92,27 +100,27 @@ def tile_contextual_position_gates_s10_kernel(
                 piece = keep.tile([P, width], BF16, name="logits%d_%d" % (m, i))
                 nc.sync.dma_start(out=piece[:], in_=logits[m * P : (m + 1) * P, i * width : (i + 1) * width])
                 for j in range(2 // pieces):
-                    logit_sb[(m, i + j)] = piece[:, j * (K // 2) : (j + 1) * (K // 2)]
+                    logit_words[(m, i + j)] = piece[:, j * (K // 2) : (j + 1) * (K // 2)].bitcast(F32)
 
         def load_far_scales():
             for row in range(4):
                 nc.sync.dma_start(
-                    out=far_sc[row:P:32, :, :].bitcast(I32),
+                    out=far_sc[row:P:QUADRANT, :, :].bitcast(I32),
                     in_=far_scales[:, row:16:4, :].rearrange("g q n -> q g n").bitcast(I32),
                 )
 
-        def load_far(b):
-            far_sb[b] = keep.tile([P, 2, 2 * N], U8, name="far%d" % b, align_bytes=64)
+        def load_far(pair):
+            far_sb[pair] = keep.tile([P, 2, 2 * N], U8, name="far%d" % pair, align_bytes=64)
             nc.sync.dma_start(
-                out=far_sb[b][:].bitcast(I32),
-                in_=far_words[2 * b : 2 * b + 2].rearrange("g p n -> p g n").bitcast(I32),
+                out=far_sb[pair][:].bitcast(I32),
+                in_=far_words[2 * pair : 2 * pair + 2].rearrange("g p n -> p g n").bitcast(I32),
             )
 
         def load_near_scales():
-            for q in range(4):
+            for quad in range(4):
                 nc.sync.dma_start(
-                    out=near_sc[32 * q : 32 * q + 16, :].bitcast(I32),
-                    in_=near_scales[:, 4 * q : 4 * q + 4, :].bitcast(I32),
+                    out=near_sc[QUADRANT * quad : QUADRANT * quad + 4 * PASSES, :].bitcast(I32),
+                    in_=near_scales[:, 4 * quad : 4 * quad + 4, :].bitcast(I32),
                 )
 
         def load_near(h):
@@ -129,7 +137,7 @@ def tile_contextual_position_gates_s10_kernel(
                 in_=mix[g * K_PASS : (g + 1) * K_PASS, cols(h)].rearrange("(p t) n -> p t n", t=PACK),
             )
 
-        r_sb = keep.tile([P, PASSES, 16], BF16, name="r_sb")
+        r_sb = keep.tile([P, PASSES, R_PITCH], BF16, name="r_sb")
         load_logits(0, 2)
         nc.sync.dma_start(out=r_sb[:, :, :PACK], in_=r.rearrange("(g p t) -> p g t", p=P, t=PACK))
         load_logits(1, 1)
@@ -137,14 +145,14 @@ def tile_contextual_position_gates_s10_kernel(
         load_far_scales()
         load_far(0)
         load_far(1)
-        load_mix(0, 0)
         load_logits(3, 1)
         load_near_scales()
         load_near(0)
+        load_logits(4, 1)
+        load_mix(0, 0)
         load_mix(0, 1)
         load_near(1)
         load_mix(0, 2)
-        load_logits(4, 1)
         load_mix(0, 3)
         for g in range(PASSES):
             load_mix(1, g)
@@ -158,28 +166,26 @@ def tile_contextual_position_gates_s10_kernel(
         gate_sc = {}
 
         def sort_words(m):
-            for b in range(2):
+            for pair in range(2):
                 ordered = stage.tile([P, 2, 2, P], F32, name="ordered", tag="ordered")
-                nc.scalar.copy(
-                    out=ordered[:], in_=logit_sb[(m, b)].bitcast(F32).rearrange("p (g c u) -> p u g c", g=2, u=2)
-                )
-                sorted_words[(m, b)] = ordered
+                nc.scalar.copy(out=ordered[:], in_=logit_words[(m, pair)].rearrange("p (g c u) -> p u g c", g=2, u=2))
+                sorted_words[(m, pair)] = ordered
 
         def turn(m, g0, count):
             bank = take_bank(("turn", m, g0))
             for u in range(2):
                 for i in range(count):
-                    g = g0 + i
-                    if (m, g // 2) in sorted_words:
-                        words = sorted_words[(m, g // 2)][:, u, g % 2, :]
+                    pair, g_in_pair = divmod(g0 + i, 2)
+                    if (m, pair) in sorted_words:
+                        words = sorted_words[(m, pair)][:, u, g_in_pair, :]
                     else:
-                        words = logit_sb[(m, g // 2)].bitcast(F32)[:, 2 * P * (g % 2) + u : 2 * P * (g % 2 + 1) : 2]
+                        words = logit_words[(m, pair)][:, 2 * P * g_in_pair + u : 2 * P * (g_in_pair + 1) : 2]
                     slot = count * u + i
                     nc.tensor.transpose(bank[:, slot * P : (slot + 1) * P], words, ident[:])
             turned[(m, g0)] = bank[:, : 2 * count * P]
 
         def sigmoid(m, g0, count):
-            sig[(m, g0)] = stage.tile([P, count * P, 2, 2], F32, name="sig", tag="sig", bufs=4)
+            sig[(m, g0)] = stage.tile([P, count * P, 2, 2], F32, name="sig", tag="sig", bufs=SIG_BUFS)
             nc.scalar.activation(
                 out=sig[(m, g0)][:],
                 in_=turned[(m, g0)].bitcast(BF16).rearrange("p (u c e) -> p c u e", u=2, e=2),
@@ -208,17 +214,9 @@ def tile_contextual_position_gates_s10_kernel(
                 gate_codes[(m, g0 + i)] = codes[:, i * P : (i + 1) * P]
                 gate_sc[(m, g0 + i)] = scales[:, i * P : (i + 1) * P]
 
-        def turn_and_sigmoid(m):
-            for g0 in (0, 2):
-                turn(m, g0, 2)
-            for g0 in (0, 2):
-                sigmoid(m, g0, 2)
-
-        def weigh_and_quantize(m):
-            for g0 in (0, 2):
-                weigh(m, g0, 2)
-            for g0 in (0, 2):
-                quantize_gate(m, g0, 2)
+        def both_pairs(step, m):
+            step(m, 0, 2)
+            step(m, 2, 2)
 
         woven = {}
         mix_codes = {}
@@ -227,8 +225,8 @@ def tile_contextual_position_gates_s10_kernel(
         def weave(h, g, copy):
             woven[(h, g)] = stage.tile([P, N_HALF, PACK], BF16, name="woven", tag="woven", align_bytes=64)
             copy(
-                out=woven[(h, g)][:].rearrange("p (c i) t -> p c t i", i=4),
-                in_=mix_raw[(h, g)][:].rearrange("p t (c i) -> p c t i", i=4),
+                out=woven[(h, g)][:].rearrange("p (c i) t -> p c t i", i=RUN),
+                in_=mix_raw[(h, g)][:].rearrange("p t (c i) -> p c t i", i=RUN),
             )
 
         def quantize_mix(h, g):
@@ -241,6 +239,7 @@ def tile_contextual_position_gates_s10_kernel(
             )
 
         sums = {}
+        result = {}
 
         def product(kind, m, h, lo=0, hi=N_HALF, passes=range(PASSES)):
             if passes[0] == 0:
@@ -272,193 +271,156 @@ def tile_contextual_position_gates_s10_kernel(
             sums[(kind, m, h)] = parked[:]
             give_back((kind, m, h))
 
-        result = {}
-
         def tanh(m, h):
             result[(m, h)] = keep.tile([P, N_HALF], F32, name="result%d_%d" % (m, h))
             nc.scalar.activation(out=result[(m, h)][:], in_=sums[("mix", m, h)], func=ACT.Tanh)
             give_back(("mix", m, h))
 
         def times_far(m, h):
-            nc.vector.tensor_tensor(
-                out=result[(m, h)][:], in0=sums[("far", m, h)], in1=result[(m, h)][:], op=ALU.mult
-            )
+            whole = result[(m, h)][:]
+            nc.vector.tensor_tensor(out=whole, in0=sums[("far", m, h)], in1=whole, op=ALU.mult)
             give_back(("far", m, h))
 
-        def plus_near(m, h, lo=0, hi=N_HALF):
+        def plus_near_and_store(m, h, lo=0, hi=N_HALF):
             part = result[(m, h)][:, lo:hi]
             nc.vector.tensor_tensor(out=part, in0=sums[("near", m, h)], in1=part, op=ALU.add)
             give_back(("near", m, h))
             nc.sync.dma_start(out=out[m * P : (m + 1) * P, h * N_HALF + lo : h * N_HALF + hi], in_=part)
 
+        def finish_two(one, other):
+            times_far(*one)
+            times_far(*other)
+            plus_near_and_store(*one)
+            plus_near_and_store(*other)
+
         on_vector = nc.vector.tensor_copy
         on_scalar = nc.scalar.copy
 
-        keep_warm()
-        turn(0, 0, 1)
-        turn(0, 1, 1)
-        turn(0, 2, 1)
-        turn(0, 3, 1)
-        sigmoid(0, 0, 1)
-        sigmoid(0, 1, 1)
-        sigmoid(0, 2, 1)
-        sigmoid(0, 3, 1)
-        keep_warm()
-        turn(1, 0, 2)
-        turn(1, 2, 2)
-        sigmoid(1, 0, 2)
-        sigmoid(1, 2, 2)
-        weigh(0, 0, 1)
-        weigh(0, 1, 1)
-        quantize_gate(0, 0, 1)
-        weigh(0, 2, 1)
-        quantize_gate(0, 1, 1)
-        weigh(0, 3, 1)
-        quantize_gate(0, 2, 1)
-        weigh(1, 0, 2)
-        quantize_gate(0, 3, 1)
-        weigh(1, 2, 2)
-        quantize_gate(1, 0, 2)
-        quantize_gate(1, 2, 2)
-        keep_warm()
-        turn(2, 0, 2)
-        turn(2, 2, 2)
-        sigmoid(2, 0, 2)
-        sigmoid(2, 2, 2)
-        keep_warm()
+        keep_warm(WARM_FIRST)
+        for g in range(PASSES):
+            turn(0, g, 1)
+        for g in range(PASSES):
+            sigmoid(0, g, 1)
+        keep_warm(WARM_BETWEEN)
+        both_pairs(turn, 1)
+        both_pairs(sigmoid, 1)
+        chunks = [(0, g, 1) for g in range(PASSES)] + [(1, 0, 2), (1, 2, 2)]
+        weigh(*chunks[0])
+        for before, chunk in zip(chunks, chunks[1:]):
+            weigh(*chunk)
+            quantize_gate(*before)
+        quantize_gate(*chunks[-1])
+        keep_warm(WARM_BETWEEN)
+        both_pairs(turn, 2)
+        both_pairs(sigmoid, 2)
+        keep_warm(WARM_BETWEEN)
         give_back("warm")
-        product("far", 0, 0, passes=range(0, 2))
-        product("far", 0, 1, passes=range(0, 2))
-        product("far", 0, 0, passes=range(2, 4))
-        product("far", 0, 1, passes=range(2, 4))
-        weigh(2, 0, 2)
-        weigh(2, 2, 2)
-        quantize_gate(2, 0, 2)
-        quantize_gate(2, 2, 2)
+
+        for passes in (range(0, 2), range(2, 4)):
+            product("far", 0, 0, passes=passes)
+            product("far", 0, 1, passes=passes)
+        both_pairs(weigh, 2)
+        both_pairs(quantize_gate, 2)
         park("far", 0, 0)
-        park("far", 0, 1)
         product("far", 1, 0)
-        product("far", 1, 1)
-        park("far", 1, 0)
         sort_words(3)
-        park("far", 1, 1)
-        weave(0, 0, on_vector)
+        park("far", 0, 1)
+        product("far", 1, 1)
+        both_pairs(turn, 3)
+        park("far", 1, 0)
+        both_pairs(sigmoid, 3)
         product("far", 2, 0)
-        turn(3, 0, 2)
-        turn(3, 2, 2)
-        sigmoid(3, 0, 2)
-        sigmoid(3, 2, 2)
-        quantize_mix(0, 0)
         product("far", 2, 1)
+        both_pairs(weigh, 3)
+        both_pairs(quantize_gate, 3)
+        sort_words(4)
+        park("far", 1, 1)
         park("far", 2, 0)
-        park("far", 2, 1)
-        weigh(3, 0, 2)
-        weigh(3, 2, 2)
-        quantize_gate(3, 0, 2)
-        quantize_gate(3, 2, 2)
+
         product("near", 0, 0)
+        both_pairs(turn, 4)
+        both_pairs(sigmoid, 4)
         product("near", 1, 0)
-        product("near", 2, 0)
+        park("far", 2, 1)
         park("near", 0, 0)
         park("near", 1, 0)
-        park("near", 2, 0)
-        weave(0, 1, on_vector)
+        weave(0, 0, on_vector)
+        product("near", 2, 0)
         product("far", 3, 1)
-        product("near", 0, 1)
+        park("near", 2, 0)
         park("far", 3, 1)
-        park("near", 0, 1)
+        weigh(4, 0, 2)
+        quantize_mix(0, 0)
+        weigh(4, 2, 2)
+        weave(0, 1, on_vector)
+        both_pairs(quantize_gate, 4)
         quantize_mix(0, 1)
-        weave(0, 2, on_vector)
-        product("near", 1, 1)
-        sort_words(4)
-        park("near", 1, 1)
-        quantize_mix(0, 2)
-        product("near", 2, 1)
-        turn(4, 0, 2)
-        turn(4, 2, 2)
-        sigmoid(4, 0, 2)
-        sigmoid(4, 2, 2)
-        weave(0, 3, on_vector)
-        park("near", 2, 1)
         product("far", 3, 0)
         product("near", 3, 0)
-        weigh(4, 0, 2)
+        weave(0, 2, on_scalar)
+        for m in range(3):
+            product("near", m, 1)
+        for m in range(3):
+            park("near", m, 1)
+        weave(0, 3, on_vector)
+        quantize_mix(0, 2)
         quantize_mix(0, 3)
-        weigh(4, 2, 2)
-        weave(1, 0, on_scalar)
-        product("mix", 3, 0)
-        quantize_gate(4, 0, 2)
-        quantize_gate(4, 2, 2)
-        tanh(3, 0)
-        product("mix", 0, 0)
-        product("mix", 1, 0)
-        product("mix", 2, 0)
+        weave(1, 0, on_vector)
         weave(1, 1, on_vector)
-        times_far(3, 0)
-        tanh(0, 0)
-        tanh(1, 0)
+        product("near", 3, 1)
+
+        product("mix", 3, 0)
+        tanh(3, 0)
         weave(1, 2, on_scalar)
         quantize_mix(1, 0)
-        plus_near(3, 0)
         quantize_mix(1, 1)
-        tanh(2, 0)
-        product("mix", 4, 0)
-        product("far", 4, 0)
-        product("near", 4, 0)
+        for m in range(3):
+            product("mix", m, 0)
+        times_far(3, 0)
         weave(1, 3, on_vector)
-        tanh(4, 0)
-        sort_words(5)
+        plus_near_and_store(3, 0)
+        for m in range(3):
+            tanh(m, 0)
         quantize_mix(1, 2)
         quantize_mix(1, 3)
-        times_far(4, 0)
-        times_far(0, 0)
-        plus_near(4, 0)
-        plus_near(0, 0)
-        product("near", 3, 1)
+        for kind in ("mix", "far", "near"):
+            product(kind, 4, 0)
+        tanh(4, 0)
+        finish_two((0, 0), (1, 0))
+        sort_words(5)
+        finish_two((4, 0), (2, 0))
+
         product("mix", 3, 1)
-        turn(5, 0, 2)
-        turn(5, 2, 2)
+        both_pairs(turn, 5)
         tanh(3, 1)
-        sigmoid(5, 0, 2)
-        sigmoid(5, 2, 2)
-        times_far(1, 0)
-        times_far(2, 0)
-        plus_near(1, 0)
-        plus_near(2, 0)
+        both_pairs(sigmoid, 5)
         product("mix", 0, 1)
         tanh(0, 1)
         times_far(3, 1)
         weigh(5, 0, 2)
-        plus_near(3, 1)
+        plus_near_and_store(3, 1)
         weigh(5, 2, 2)
-        quantize_gate(5, 0, 2)
-        quantize_gate(5, 2, 2)
+        both_pairs(quantize_gate, 5)
         product("mix", 4, 1)
         tanh(4, 1)
         product("far", 4, 1)
         product("near", 4, 1)
-        times_far(0, 1)
-        times_far(4, 1)
-        plus_near(0, 1)
-        plus_near(4, 1)
-        product("mix", 1, 1)
-        tanh(1, 1)
-        product("mix", 2, 1)
-        tanh(2, 1)
+        finish_two((0, 1), (4, 1))
+        for m in (1, 2):
+            product("mix", m, 1)
+            tanh(m, 1)
+
         product("mix", 5, 0)
         tanh(5, 0)
-        times_far(1, 1)
-        times_far(2, 1)
-        plus_near(1, 1)
-        plus_near(2, 1)
+        finish_two((1, 1), (2, 1))
         product("far", 5, 0)
         product("near", 5, 0)
         times_far(5, 0)
         product("mix", 5, 1)
-        plus_near(5, 0)
+        plus_near_and_store(5, 0)
         tanh(5, 1)
         product("far", 5, 1)
         times_far(5, 1)
         for lo in (0, N_HALF // 2):
             product("near", 5, 1, lo, lo + N_HALF // 2)
-            plus_near(5, 1, lo, lo + N_HALF // 2)
+            plus_near_and_store(5, 1, lo, lo + N_HALF // 2)

from contextlib import ExitStack

import concourse.mybir as mybir
from concourse.masks import make_identity

M, K, N = 768, 2048, 1024
FLOPS = 3 * 2 * M * K * N

F32 = mybir.dt.float32
BF16 = mybir.dt.bfloat16
I32 = mybir.dt.int32
U32 = mybir.dt.uint32
U8 = mybir.dt.uint8
FP8X4 = mybir.dt.float8_e4m3fn_x4
FP4X4 = mybir.dt.float4_e2m1fn_x4
ACT = mybir.ActivationFunctionType
ALU = mybir.AluOpType

P = 128
PACK = 4
K_PASS = P * PACK
PASSES = K // K_PASS
N_HALF = 512
BANKS = 8
QUADRANT = 32
R_PITCH = 16
RUN = 4
STAGE_BUFS = 3
SIG_BUFS = 4
WARM_N = 256
WARM_FIRST = 5
WARM_BETWEEN = 4
ONES_BF16_PAIR = 0x3F803F80


def tile_contextual_position_gates_s10_kernel(
    tc, logits, r, far_words, far_scales, near_words, near_scales, mix, out
):
    nc = tc.nc
    with ExitStack() as ctx:
        keep = ctx.enter_context(tc.tile_pool(name="keep", bufs=1))
        stage = ctx.enter_context(tc.tile_pool(name="stage", bufs=STAGE_BUFS))
        psum = ctx.enter_context(tc.psum_pool(name="psum", bufs=1))
        ctx.enter_context(tc.manual_schedule())

        free_banks = ["bank%d" % i for i in range(BANKS)]
        bank_of = {}

        def take_bank(key):
            tag = free_banks[0]
            free_banks.remove(tag)
            bank_of[key] = tag
            bank = psum.tile([P, N_HALF], F32, name=tag, tag=tag)
            return bank

        def give_back(key):
            if bank_of[key]:
                free_banks.append(bank_of[key])
                bank_of[key] = None

        def cols(h):
            return slice(h * N_HALF, (h + 1) * N_HALF)

        ones = keep.tile([P, PACK * WARM_N], BF16, name="ones", align_bytes=64)
        warm_codes = keep.tile([P, WARM_N], U32, name="warm_codes", align_bytes=64)
        warm_sc = keep.tile([P, WARM_N], U8, name="warm_sc", align_bytes=64)
        nc.vector.memset(ones[:].bitcast(I32), ONES_BF16_PAIR)
        nc.vector.quantize_mx(out=warm_codes[:].bitcast(FP8X4), scales=warm_sc[:], in_=ones[:])
        warm_bank = take_bank("warm")

        def keep_warm(count):
            for i in range(count):
                nc.tensor.matmul_mx(
                    out=warm_bank[:, :WARM_N],
                    lhsT=warm_codes[:, :P].bitcast(FP8X4),
                    lhsT_scale=warm_sc[:, :P],
                    rhs=warm_codes[:].bitcast(FP8X4),
                    rhs_scale=warm_sc[:],
                    start=True,
                    stop=True,
                )

        ident = keep.tile([P, P], F32, name="ident")
        nc.vector.memset(ident[:], 0.0)
        make_identity(nc, ident[:], nomemset=True)

        far_sc = keep.tile([P, PASSES, N], U8, name="far_sc", align_bytes=64)
        near_sc = keep.tile([P, N], U8, name="near_sc", align_bytes=64)
        nc.vector.memset(far_sc[:].bitcast(I32), 0)
        nc.vector.memset(near_sc[:].bitcast(I32), 0)

        logit_words = {}
        far_sb = {}
        near_sb = {}
        mix_raw = {}

        def load_logits(m, pieces):
            width = K // pieces
            for i in range(pieces):
                piece = keep.tile([P, width], BF16, name="logits%d_%d" % (m, i))
                nc.sync.dma_start(out=piece[:], in_=logits[m * P : (m + 1) * P, i * width : (i + 1) * width])
                for j in range(2 // pieces):
                    logit_words[(m, i + j)] = piece[:, j * (K // 2) : (j + 1) * (K // 2)].bitcast(F32)

        def load_far_scales():
            for row in range(4):
                nc.sync.dma_start(
                    out=far_sc[row:P:QUADRANT, :, :].bitcast(I32),
                    in_=far_scales[:, row:16:4, :].rearrange("g q n -> q g n").bitcast(I32),
                )

        def load_far(pair):
            far_sb[pair] = keep.tile([P, 2, 2 * N], U8, name="far%d" % pair, align_bytes=64)
            nc.sync.dma_start(
                out=far_sb[pair][:].bitcast(I32),
                in_=far_words[2 * pair : 2 * pair + 2].rearrange("g p n -> p g n").bitcast(I32),
            )

        def load_near_scales():
            for quad in range(4):
                nc.sync.dma_start(
                    out=near_sc[QUADRANT * quad : QUADRANT * quad + 4 * PASSES, :].bitcast(I32),
                    in_=near_scales[:, 4 * quad : 4 * quad + 4, :].bitcast(I32),
                )

        def load_near(h):
            near_sb[h] = keep.tile([P, PASSES, N_HALF], U32, name="near%d" % h, align_bytes=64)
            nc.sync.dma_start(
                out=near_sb[h][:].bitcast(I32),
                in_=near_words[:, :, cols(h), :].rearrange("g p n t -> p g (n t)").bitcast(I32),
            )

        def load_mix(h, g):
            mix_raw[(h, g)] = keep.tile([P, PACK, N_HALF], BF16, name="mix%d_%d" % (h, g))
            nc.sync.dma_start(
                out=mix_raw[(h, g)][:],
                in_=mix[g * K_PASS : (g + 1) * K_PASS, cols(h)].rearrange("(p t) n -> p t n", t=PACK),
            )

        r_sb = keep.tile([P, PASSES, R_PITCH], BF16, name="r_sb")
        load_logits(0, 2)
        nc.sync.dma_start(out=r_sb[:, :, :PACK], in_=r.rearrange("(g p t) -> p g t", p=P, t=PACK))
        load_logits(1, 1)
        load_logits(2, 1)
        load_far_scales()
        load_far(0)
        load_far(1)
        load_logits(3, 1)
        load_near_scales()
        load_near(0)
        load_logits(4, 1)
        load_mix(0, 0)
        load_mix(0, 1)
        load_near(1)
        load_mix(0, 2)
        load_mix(0, 3)
        for g in range(PASSES):
            load_mix(1, g)
        load_logits(5, 1)

        sorted_words = {}
        turned = {}
        sig = {}
        gate_bf = {}
        gate_codes = {}
        gate_sc = {}

        def sort_words(m):
            for pair in range(2):
                ordered = stage.tile([P, 2, 2, P], F32, name="ordered", tag="ordered")
                nc.scalar.copy(out=ordered[:], in_=logit_words[(m, pair)].rearrange("p (g c u) -> p u g c", g=2, u=2))
                sorted_words[(m, pair)] = ordered

        def turn(m, g0, count):
            bank = take_bank(("turn", m, g0))
            for u in range(2):
                for i in range(count):
                    pair, g_in_pair = divmod(g0 + i, 2)
                    if (m, pair) in sorted_words:
                        words = sorted_words[(m, pair)][:, u, g_in_pair, :]
                    else:
                        words = logit_words[(m, pair)][:, 2 * P * g_in_pair + u : 2 * P * (g_in_pair + 1) : 2]
                    slot = count * u + i
                    nc.tensor.transpose(bank[:, slot * P : (slot + 1) * P], words, ident[:])
            turned[(m, g0)] = bank[:, : 2 * count * P]

        def sigmoid(m, g0, count):
            sig[(m, g0)] = stage.tile([P, count * P, 2, 2], F32, name="sig", tag="sig", bufs=SIG_BUFS)
            nc.scalar.activation(
                out=sig[(m, g0)][:],
                in_=turned[(m, g0)].bitcast(BF16).rearrange("p (u c e) -> p c u e", u=2, e=2),
                func=ACT.Sigmoid,
            )
            give_back(("turn", m, g0))

        def weigh(m, g0, count):
            gate_bf[(m, g0)] = stage.tile([P, count, P, PACK], BF16, name="gate_bf", tag="gate_bf", align_bytes=64)
            nc.vector.tensor_tensor(
                out=gate_bf[(m, g0)][:],
                in0=sig[(m, g0)][:].rearrange("p (g c) u e -> p g c (u e)", g=count),
                in1=r_sb[:, g0 : g0 + count, :PACK].unsqueeze(2).to_broadcast([P, count, P, PACK]),
                op=ALU.mult,
            )

        def quantize_gate(m, g0, count):
            codes = keep.tile([P, count * P], U32, name="gate_codes%d_%d" % (m, g0), align_bytes=64)
            scales = keep.tile([P, count * P], U8, name="gate_sc%d_%d" % (m, g0), align_bytes=64)
            nc.vector.quantize_mx(
                out=codes[:].bitcast(FP8X4),
                scales=scales[:],
                in_=gate_bf[(m, g0)][:].rearrange("p g c t -> p (g c t)"),
            )
            for i in range(count):
                gate_codes[(m, g0 + i)] = codes[:, i * P : (i + 1) * P]
                gate_sc[(m, g0 + i)] = scales[:, i * P : (i + 1) * P]

        def both_pairs(step, m):
            step(m, 0, 2)
            step(m, 2, 2)

        woven = {}
        mix_codes = {}
        mix_sc = {}

        def weave(h, g, copy):
            woven[(h, g)] = stage.tile([P, N_HALF, PACK], BF16, name="woven", tag="woven", align_bytes=64)
            copy(
                out=woven[(h, g)][:].rearrange("p (c i) t -> p c t i", i=RUN),
                in_=mix_raw[(h, g)][:].rearrange("p t (c i) -> p c t i", i=RUN),
            )

        def quantize_mix(h, g):
            mix_codes[(h, g)] = keep.tile([P, N_HALF], U32, name="mix_codes%d_%d" % (h, g), align_bytes=64)
            mix_sc[(h, g)] = keep.tile([P, N_HALF], U8, name="mix_sc%d_%d" % (h, g), align_bytes=64)
            nc.vector.quantize_mx(
                out=mix_codes[(h, g)][:].bitcast(FP8X4),
                scales=mix_sc[(h, g)][:],
                in_=woven[(h, g)][:].rearrange("p c t -> p (c t)"),
            )

        sums = {}
        result = {}

        def product(kind, m, h, lo=0, hi=N_HALF, passes=range(PASSES)):
            if passes[0] == 0:
                sums[(kind, m, h)] = take_bank((kind, m, h))[:, : hi - lo]
            first, last = h * N_HALF + lo, h * N_HALF + hi
            for g in passes:
                if kind == "far":
                    rhs = far_sb[g // 2][:, g % 2, 2 * first : 2 * last].bitcast(FP4X4)
                    rhs_scale = far_sc[:, g, first:last]
                elif kind == "near":
                    rhs = near_sb[h][:, g, lo:hi].bitcast(FP8X4)
                    rhs_scale = near_sc[4 * g : P, first:last]
                else:
                    rhs = mix_codes[(h, g)][:, lo:hi].bitcast(FP8X4)
                    rhs_scale = mix_sc[(h, g)][:, lo:hi]
                nc.tensor.matmul_mx(
                    out=sums[(kind, m, h)],
                    lhsT=gate_codes[(m, g)].bitcast(FP8X4),
                    lhsT_scale=gate_sc[(m, g)],
                    rhs=rhs,
                    rhs_scale=rhs_scale,
                    start=(g == 0),
                    stop=(g == PASSES - 1),
                )

        def park(kind, m, h):
            parked = keep.tile([P, N_HALF], F32, name="parked_%s%d_%d" % (kind, m, h))
            nc.scalar.copy(out=parked[:], in_=sums[(kind, m, h)])
            sums[(kind, m, h)] = parked[:]
            give_back((kind, m, h))

        def tanh(m, h):
            result[(m, h)] = keep.tile([P, N_HALF], F32, name="result%d_%d" % (m, h))
            nc.scalar.activation(out=result[(m, h)][:], in_=sums[("mix", m, h)], func=ACT.Tanh)
            give_back(("mix", m, h))

        def times_far(m, h):
            whole = result[(m, h)][:]
            nc.vector.tensor_tensor(out=whole, in0=sums[("far", m, h)], in1=whole, op=ALU.mult)
            give_back(("far", m, h))

        def plus_near_and_store(m, h, lo=0, hi=N_HALF):
            part = result[(m, h)][:, lo:hi]
            nc.vector.tensor_tensor(out=part, in0=sums[("near", m, h)], in1=part, op=ALU.add)
            give_back(("near", m, h))
            nc.sync.dma_start(out=out[m * P : (m + 1) * P, h * N_HALF + lo : h * N_HALF + hi], in_=part)

        def finish_two(one, other):
            times_far(*one)
            times_far(*other)
            plus_near_and_store(*one)
            plus_near_and_store(*other)

        on_vector = nc.vector.tensor_copy
        on_scalar = nc.scalar.copy

        keep_warm(WARM_FIRST)
        for g in range(PASSES):
            turn(0, g, 1)
        for g in range(PASSES):
            sigmoid(0, g, 1)
        keep_warm(WARM_BETWEEN)
        both_pairs(turn, 1)
        both_pairs(sigmoid, 1)
        chunks = [(0, g, 1) for g in range(PASSES)] + [(1, 0, 2), (1, 2, 2)]
        weigh(*chunks[0])
        for before, chunk in zip(chunks, chunks[1:]):
            weigh(*chunk)
            quantize_gate(*before)
        quantize_gate(*chunks[-1])
        keep_warm(WARM_BETWEEN)
        both_pairs(turn, 2)
        both_pairs(sigmoid, 2)
        keep_warm(WARM_BETWEEN)
        give_back("warm")

        for passes in (range(0, 2), range(2, 4)):
            product("far", 0, 0, passes=passes)
            product("far", 0, 1, passes=passes)
        both_pairs(weigh, 2)
        both_pairs(quantize_gate, 2)
        park("far", 0, 0)
        product("far", 1, 0)
        sort_words(3)
        park("far", 0, 1)
        product("far", 1, 1)
        both_pairs(turn, 3)
        park("far", 1, 0)
        both_pairs(sigmoid, 3)
        product("far", 2, 0)
        product("far", 2, 1)
        both_pairs(weigh, 3)
        both_pairs(quantize_gate, 3)
        sort_words(4)
        park("far", 1, 1)
        park("far", 2, 0)

        product("near", 0, 0)
        both_pairs(turn, 4)
        both_pairs(sigmoid, 4)
        product("near", 1, 0)
        park("far", 2, 1)
        park("near", 0, 0)
        park("near", 1, 0)
        weave(0, 0, on_vector)
        product("near", 2, 0)
        product("far", 3, 1)
        park("near", 2, 0)
        park("far", 3, 1)
        weigh(4, 0, 2)
        quantize_mix(0, 0)
        weigh(4, 2, 2)
        weave(0, 1, on_vector)
        both_pairs(quantize_gate, 4)
        quantize_mix(0, 1)
        product("far", 3, 0)
        product("near", 3, 0)
        weave(0, 2, on_scalar)
        for m in range(3):
            product("near", m, 1)
        for m in range(3):
            park("near", m, 1)
        weave(0, 3, on_vector)
        quantize_mix(0, 2)
        quantize_mix(0, 3)
        weave(1, 0, on_vector)
        weave(1, 1, on_vector)
        product("near", 3, 1)

        product("mix", 3, 0)
        tanh(3, 0)
        weave(1, 2, on_scalar)
        quantize_mix(1, 0)
        quantize_mix(1, 1)
        for m in range(3):
            product("mix", m, 0)
        times_far(3, 0)
        weave(1, 3, on_vector)
        plus_near_and_store(3, 0)
        for m in range(3):
            tanh(m, 0)
        quantize_mix(1, 2)
        quantize_mix(1, 3)
        for kind in ("mix", "far", "near"):
            product(kind, 4, 0)
        tanh(4, 0)
        finish_two((0, 0), (1, 0))
        sort_words(5)
        finish_two((4, 0), (2, 0))

        product("mix", 3, 1)
        both_pairs(turn, 5)
        tanh(3, 1)
        both_pairs(sigmoid, 5)
        product("mix", 0, 1)
        tanh(0, 1)
        times_far(3, 1)
        weigh(5, 0, 2)
        plus_near_and_store(3, 1)
        weigh(5, 2, 2)
        both_pairs(quantize_gate, 5)
        product("mix", 4, 1)
        tanh(4, 1)
        product("far", 4, 1)
        product("near", 4, 1)
        finish_two((0, 1), (4, 1))
        for m in (1, 2):
            product("mix", m, 1)
            tanh(m, 1)

        product("mix", 5, 0)
        tanh(5, 0)
        finish_two((1, 1), (2, 1))
        product("far", 5, 0)
        product("near", 5, 0)
        times_far(5, 0)
        product("mix", 5, 1)
        plus_near_and_store(5, 0)
        tanh(5, 1)
        product("far", 5, 1)
        times_far(5, 1)
        for lo in (0, N_HALF // 2):
            product("near", 5, 1, lo, lo + N_HALF // 2)
            plus_near_and_store(5, 1, lo, lo + N_HALF // 2)
